import numpy as np, ml_dtypes
CORES = [1,17,65,89,97,113]
N = 6
KT, HT, TK = 1, 2, 64
def setup_inputs(rng):
    w = (rng.standard_normal((128, KT * HT * 128), dtype=np.float32) / 8).astype(ml_dtypes.bfloat16)
    return {"x": rng.standard_normal((N, 128, KT * TK), dtype=np.float32).astype(ml_dtypes.bfloat16), "w": np.broadcast_to(w, (N,) + w.shape).copy()}
def setup_inputs_big(rng):
    d = setup_inputs(rng)
    for k in ("x", "w"): d[k] = (d[k].astype(np.float32) * 1024.0).astype(d[k].dtype)
    return d
def setup_inputs_small(rng):
    d = setup_inputs(rng)
    for k in ("x", "w"): d[k] = (d[k].astype(np.float32) * (1 / 1024.0)).astype(d[k].dtype)
    return d
def setup_inputs_apart(rng):
    d = setup_inputs(rng)
    f = (10.0 ** rng.permutation(np.linspace(-1.5, 1.5, N))).astype(np.float32).reshape(N, 1, 1)
    for k in ("x",): d[k] = (d[k].astype(np.float32) * f).astype(d[k].dtype)
    return d
def tie_inputs(x):
    x = dict(x)
    x["w"] = np.broadcast_to(x["w"][0], x["w"].shape).copy()
    return x
def reference(x, w):
    X, W = x.astype(np.float64), w.astype(np.float64)
    def hidden(r):
        return np.stack([np.maximum(sum(W[r][:, 128 * (HT * t + u):128 * (HT * t + u) + 128].T @ X[r][:, TK * t:TK * t + TK] for t in range(KT)), 0.0) for u in range(HT)])
    h = [hidden(r) for r in range(N)]
    y = np.stack([sum(h[(r - 1) % N][u].T @ h[r][u] for u in range(HT)) for r in range(N)])
    return {"y": y.astype(ml_dtypes.bfloat16 if x.dtype != np.float64 else np.float64)}

from concourse.mybir import AluOpType

TK = 64
HT = 2
BANK = 512

SCRATCH = {
    "xd": ("dram", [128, TK], "bfloat16"),
    "rd": ("dram", [128, TK], "bfloat16"),
    "xs": ("sbuf", [128, TK], "bfloat16"),
    "xp": ("sbuf", [128, TK], "bfloat16"),
    "ws": ("sbuf", [128, HT * 128], "bfloat16"),
    "zero": ("sbuf", [128, TK], "float32"),
    "hr": ("sbuf", [128, HT * TK], "bfloat16"),
    "hp": ("sbuf", [128, HT * TK], "bfloat16"),
    "ys": ("sbuf", [128, TK], "bfloat16"),
    "pr0": ("psum", [128, BANK], "float32"),
    "pr1": ("psum", [128, BANK], "float32"),
    "pp0": ("psum", [128, BANK], "float32"),
    "pp1": ("psum", [128, BANK], "float32"),
    "py": ("psum", [128, BANK], "float32"),
}
SEMAPHORES = ["xd_ok", "in_ok", "w_ok", "zero_ok", "sent", "passing", "arrived",
              "mr0", "mr1", "hr_ok", "mp0", "mp1", "hp0", "hp1", "y_ok", "ys_ok", "stored"]

ENG_LONG = 4
ENG_SBUF = 8


def _engines(topo, src, dst, n):
    full = topo.mask(src, dst)
    bits = [b for b in range(full.bit_length()) if (full >> b) & 1]
    n = min(n, len(bits))
    step = len(bits) // n
    m = 0
    for b in bits[::step][:n]:
        m |= 1 << b
    return m, n


def _route(T, topo, src, dst):
    if topo.may_write(src, dst):
        return [src, dst]
    group = list(T.cores)
    near = [c for c in range(topo.CHIPS * topo.CORES_PER_CHIP)
            if topo.chip(c) == topo.chip(src) and c not in group and topo.may_write(c, dst)]
    same_die = [c for c in near if topo.die(c) == topo.die(src)]
    return [src, (same_die or near)[0], dst]


def _send(g, T, topo, src, dst, out, in_, sem, n):
    rid, pid, _ = topo.addr(dst)
    mask, n = _engines(topo, src, dst, n)
    g.remote_dma(out_ap=out, in_ap=in_, remote_sem=sem, local_sem=T.sem.sent,
                 pid=pid, routing_id=rid, dma_engine_mask=mask)
    return n


def rank_program(g, core, T, topo):
    cores = list(T.cores)
    n_ranks = len(cores)
    routes = [_route(T, topo, cores[i], cores[(i + 1) % n_ranks]) for i in range(n_ranks)]
    rank = T.rank_of(core)

    if rank is None:
        for way in routes:
            if len(way) == 3 and way[1] == core:
                _, n_in = _engines(topo, way[0], core, ENG_LONG)
                g.wait_ge(T.sem.passing, n_in)
                n = _send(g, T, topo, core, way[2], T.xp[:], T.rd[:], T.sem.arrived, ENG_SBUF)
                g.wait_ge(T.sem.sent, n)
        return

    S = T.sem
    g.sync.dma_start(T.xd[:], T.x[:]).then_inc(S.xd_ok, 16)
    g.scalar.dma_start(T.ws[:], T.w[:]).then_inc(S.w_ok, 16)
    g.sync.dma_start(T.xs[:], T.x[:]).then_inc(S.in_ok, 16)
    g.vector.memset(T.zero[:], 0.0).then_inc(S.zero_ok, 1)

    way = routes[rank]
    g.wait_ge(S.xd_ok, 16)
    if len(way) == 2:
        n = _send(g, T, topo, core, way[1], T.xp[:], T.xd[:], S.arrived, ENG_SBUF)
    else:
        n = _send(g, T, topo, core, way[1], T.rd[:], T.xd[:], S.passing, ENG_LONG)
    g.wait_ge(S.sent, n)

    back = routes[(rank - 1) % n_ranks]
    _, n_arr = _engines(topo, back[-2], core, ENG_SBUF)

    te, ve = g.tensor, g.vector
    w_tile = [T.ws[:, 128 * u:128 * (u + 1)] for u in range(HT)]
    col = [slice(TK * u, TK * (u + 1)) for u in range(HT)]

    te.wait_ge(S.w_ok, 16)
    te.wait_ge(S.in_ok, 16)
    te.matmul(T.pr0[:, 0:TK], w_tile[0], T.xs[:], start=True, stop=True).then_inc(S.mr0, 1)
    te.matmul(T.pr1[:, 0:TK], w_tile[1], T.xs[:], start=True, stop=True).then_inc(S.mr1, 1)
    te.wait_ge(S.arrived, n_arr)
    te.matmul(T.pp0[:, 0:TK], w_tile[0], T.xp[:], start=True, stop=True).then_inc(S.mp0, 1)
    te.matmul(T.pp1[:, 0:TK], w_tile[1], T.xp[:], start=True, stop=True).then_inc(S.mp1, 1)
    te.wait_ge(S.hr_ok, 2)
    te.wait_ge(S.hp0, 1)
    te.matmul(T.py[0:TK, 0:TK], T.hp[:, col[0]], T.hr[:, col[0]], start=True, stop=False)
    te.wait_ge(S.hp1, 1)
    te.matmul(T.py[0:TK, 0:TK], T.hp[:, col[1]], T.hr[:, col[1]], start=False, stop=True).then_inc(S.y_ok, 1)

    ve.wait_ge(S.zero_ok, 1)
    ve.wait_ge(S.mr0, 1)
    ve.tensor_tensor(T.hr[:, col[0]], T.pr0[:, 0:TK], T.zero[:], AluOpType.max).then_inc(S.hr_ok, 1)
    ve.wait_ge(S.mr1, 1)
    ve.tensor_tensor(T.hr[:, col[1]], T.pr1[:, 0:TK], T.zero[:], AluOpType.max).then_inc(S.hr_ok, 1)
    ve.wait_ge(S.mp0, 1)
    ve.tensor_tensor(T.hp[:, col[0]], T.pp0[:, 0:TK], T.zero[:], AluOpType.max).then_inc(S.hp0, 1)
    ve.wait_ge(S.mp1, 1)
    ve.tensor_tensor(T.hp[:, col[1]], T.pp1[:, 0:TK], T.zero[:], AluOpType.max).then_inc(S.hp1, 1)
    ve.wait_ge(S.y_ok, 1)
    ve.tensor_copy(T.ys[0:TK, :], T.py[0:TK, 0:TK]).then_inc(S.ys_ok, 1)

    g.sync.wait_ge(S.ys_ok, 1)
    g.sync.dma_start(T.y[:], T.ys[0:TK, :]).then_inc(S.stored, 16)
    g.sync.wait_ge(S.stored, 16)
